import numpy as np
import ml_dtypes


def mxq(x, axis, fmt="e4m3"):
    dtype, down = {"e4m3": (ml_dtypes.float8_e4m3fn, 7), "e5m2": (ml_dtypes.float8_e5m2, 14)}[fmt]
    v = np.moveaxis(np.asarray(x, np.float32).astype(ml_dtypes.bfloat16).astype(np.float64), axis, -1)
    blocks = v.reshape(v.shape[:-1] + (-1, 32))
    amax = np.abs(blocks).max(-1, keepdims=True)
    byte = np.maximum(np.where(amax > 0, np.frexp(amax)[1] - 1 + 127, 0) - down, 1)
    scale = np.exp2(byte - 127.0)
    codes = (blocks / scale).astype(np.float32).astype(dtype).astype(np.float64)
    return np.moveaxis((codes * scale).reshape(v.shape), -1, axis)


WIDE = False


def mx_kscale(k):
    if not WIDE:
        return np.ones(k)
    levels = np.array([10, -10, 5, -5, 0])
    if k % 512:
        return np.exp2(np.random.permutation(np.resize(levels, k // 32))).repeat(32)
    a = np.empty((k // 512, 16))
    for p in range(k // 512):
        a[p, :8] = np.random.permutation(np.resize(levels, 8))
        for g in range(8):
            far = levels[np.abs(levels - a[p, g]) >= 10]
            a[p, g + 8] = far[np.random.randint(len(far))]
    return np.exp2(a.ravel()).repeat(32)


def f64(x):
    return np.asarray(x).astype(np.float64)


def striped(idx):
    return np.tile(idx.reshape(-1, 16).T, (8, 1)).astype(np.uint16)


def unstriped(offs):
    return offs[:16].T.reshape(-1).astype(np.int64)


def silu(v):
    return v / (1.0 + np.exp(-np.maximum(v, -700.0)))


K, T, S, N = 512, 4096, 1024, 128


def setup_inputs():
    n = np.random.standard_normal
    s = mx_kscale(K)[:, None]
    return {
        "xT": (n((K, T)) * s).astype(np.float32),
        "side": n((N, T)).astype(np.float32),
        "w1": (n((K, N)) / np.sqrt(K) / s).astype(np.float32),
        "offs": striped(np.random.permutation(T)[:S]),
    }


def reference(xT, side, w1, offs):
    xq = mxq(f64(xT)[:, unstriped(offs)], 0, "e4m3")
    y = mxq(f64(w1), 0, "e4m3").T @ xq
    g = f64(side)[:, unstriped(offs)]
    return y * silu(g)

@@ -1,0 +1,93 @@
+from contextlib import ExitStack
+
+import concourse.mybir as mybir
+
+K, T, S, N = 512, 4096, 1024, 128
+FLOPS = 2 * K * S * N
+
+F32 = mybir.dt.float32
+BF16 = mybir.dt.bfloat16
+U32 = mybir.dt.uint32
+U16 = mybir.dt.uint16
+U8 = mybir.dt.uint8
+FP8X4 = mybir.dt.float8_e4m3fn_x4
+SILU = mybir.ActivationFunctionType.Silu
+MULT = mybir.AluOpType.mult
+
+P = 128
+PACK = 4
+GROUP = 16
+HALF = 512
+PIECES = ((0, 512), (512, 768), (768, 1024))
+
+
+def tile_picked_sidegate_silu_l_kernel(tc, xT, side, w1, offs, out):
+    nc = tc.nc
+    with ExitStack() as ctx:
+        keep = ctx.enter_context(tc.tile_pool(name="keep", bufs=1))
+        psum = ctx.enter_context(tc.psum_pool(name="psum", bufs=1))
+
+        offsets = keep.tile([P, S // GROUP], U16, name="offsets")
+        x_rows = xT.rearrange("(p j) t -> p j t", j=PACK)
+        planes = [keep.tile([P, T], F32, name=f"plane{j}") for j in range(PACK)]
+        w_raw = keep.tile([P, PACK, N], F32, name="w_raw")
+        side_rows = keep.tile([P, T], F32, name="side_rows")
+
+        nc.sync.dma_start(out=planes[0][:], in_=x_rows[:, 0, :])
+        nc.sync.dma_start(offsets[:], offs)
+        for j in range(1, PACK):
+            nc.sync.dma_start(out=planes[j][:], in_=x_rows[:, j, :])
+        nc.sync.dma_start(out=w_raw[:], in_=w1.rearrange("(p j) m -> p j m", j=PACK))
+        nc.sync.dma_start(out=side_rows[:], in_=side)
+
+        x_grouped = keep.tile([P, S, PACK], BF16, name="x_grouped", align_bytes=64)
+        for j in range(PACK):
+            nc.vector.tensor_copy(x_grouped[:, :, j], planes[j][:].indirect(offsets[:]))
+
+        w_grouped = keep.tile([P, N, PACK], BF16, name="w_grouped", align_bytes=64)
+        nc.scalar.copy(out=w_grouped[:], in_=w_raw[:].rearrange("p j m -> p m j"))
+        w_codes = keep.tile([P, N], U32, name="w_codes", align_bytes=64)
+        w_scales = keep.tile([P, N], U8, name="w_scales", align_bytes=64)
+        nc.vector.quantize_mx(
+            out=w_codes[:].bitcast(FP8X4),
+            scales=w_scales[:],
+            in_=w_grouped[:].rearrange("p m j -> p (m j)"),
+        )
+        x_codes = keep.tile([P, S], U32, name="x_codes", align_bytes=64)
+        x_scales = keep.tile([P, S], U8, name="x_scales", align_bytes=64)
+        nc.vector.quantize_mx(
+            out=x_codes[:].bitcast(FP8X4),
+            scales=x_scales[:],
+            in_=x_grouped[:].rearrange("p s j -> p (s j)"),
+        )
+
+        banks = []
+        for h in range(S // HALF):
+            cols = slice(h * HALF, (h + 1) * HALF)
+            bank = psum.tile([P, HALF], F32, name=f"bank{h}")
+            nc.tensor.matmul_mx(
+                out=bank[:],
+                lhsT=w_codes[:].bitcast(FP8X4),
+                lhsT_scale=w_scales[:],
+                rhs=x_codes[:, cols].bitcast(FP8X4),
+                rhs_scale=x_scales[:, cols],
+                start=True,
+                stop=True,
+            )
+            banks.append(bank)
+
+        picked = []
+        for h in range(S // HALF):
+            g = keep.tile([P, HALF], F32, name=f"picked{h}")
+            lo = h * HALF // GROUP
+            nc.vector.tensor_copy(g[:], side_rows[:].indirect(offsets[:, lo : lo + HALF // GROUP]))
+            picked.append(g)
+
+        for lo, hi in PIECES:
+            h = lo // HALF
+            cols = slice(lo - h * HALF, hi - h * HALF)
+            gate = keep.tile([P, hi - lo], F32, name=f"gate{lo}")
+            nc.scalar.activation(gate[:], picked[h][:, cols], SILU)
+            res = keep.tile([P, hi - lo], F32, name=f"res{lo}")
+            nc.vector.tensor_tensor(res[:], banks[h][:, cols], gate[:], MULT)
+            nc.sync.dma_start(out=out[:, lo:hi], in_=res[:])

@@ -18,7 +18,7 @@ P = 128
 PACK = 4
 GROUP = 16
 HALF = 512
-PIECES = ((0, 512), (512, 768), (768, 1024))
+PIECE = 256
 
 
 def tile_picked_sidegate_silu_l_kernel(tc, xT, side, w1, offs, out):
@@ -40,12 +40,34 @@ def tile_picked_sidegate_silu_l_kernel(tc, xT, side, w1, offs, out):
         nc.sync.dma_start(out=w_raw[:], in_=w1.rearrange("(p j) m -> p j m", j=PACK))
         nc.sync.dma_start(out=side_rows[:], in_=side)
 
-        x_grouped = keep.tile([P, S, PACK], BF16, name="x_grouped", align_bytes=64)
-        for j in range(PACK):
-            nc.vector.tensor_copy(x_grouped[:, :, j], planes[j][:].indirect(offsets[:]))
+        warm_in = keep.tile([P, 1], F32, name="warm_in")
+        nc.vector.memset(warm_in[:], 0.0)
+        warm_out = keep.tile([P, 1], F32, name="warm_out")
+        nc.scalar.activation(warm_out[:], warm_in[:], SILU)
 
+        halves = [offsets[:, h * HALF // GROUP : (h + 1) * HALF // GROUP] for h in range(2)]
+        grouped = [keep.tile([P, HALF, PACK], BF16, name=f"grouped{h}", align_bytes=64) for h in range(2)]
+        late_pair = keep.tile([P, 2, HALF], F32, name="late_pair")
+        for j in range(PACK):
+            if j < 2:
+                nc.vector.tensor_copy(grouped[1][:, :, j], planes[j][:].indirect(halves[1]))
+            else:
+                nc.vector.tensor_copy(late_pair[:, j - 2, :], planes[j][:].indirect(halves[1]))
+            nc.vector.tensor_copy(grouped[0][:, :, j], planes[j][:].indirect(halves[0]))
+
+        nc.scalar.copy(out=grouped[1][:, :, 2:4], in_=late_pair[:].rearrange("p j s -> p s j"))
         w_grouped = keep.tile([P, N, PACK], BF16, name="w_grouped", align_bytes=64)
         nc.scalar.copy(out=w_grouped[:], in_=w_raw[:].rearrange("p j m -> p m j"))
+
+        x_codes = keep.tile([P, S], U32, name="x_codes", align_bytes=64)
+        x_scales = keep.tile([P, S], U8, name="x_scales", align_bytes=64)
+        for h in range(2):
+            cols = slice(h * HALF, (h + 1) * HALF)
+            nc.vector.quantize_mx(
+                out=x_codes[:, cols].bitcast(FP8X4),
+                scales=x_scales[:, cols],
+                in_=grouped[h][:].rearrange("p s j -> p (s j)"),
+            )
         w_codes = keep.tile([P, N], U32, name="w_codes", align_bytes=64)
         w_scales = keep.tile([P, N], U8, name="w_scales", align_bytes=64)
         nc.vector.quantize_mx(
@@ -53,16 +75,9 @@ def tile_picked_sidegate_silu_l_kernel(tc, xT, side, w1, offs, out):
             scales=w_scales[:],
             in_=w_grouped[:].rearrange("p m j -> p (m j)"),
         )
-        x_codes = keep.tile([P, S], U32, name="x_codes", align_bytes=64)
-        x_scales = keep.tile([P, S], U8, name="x_scales", align_bytes=64)
-        nc.vector.quantize_mx(
-            out=x_codes[:].bitcast(FP8X4),
-            scales=x_scales[:],
-            in_=x_grouped[:].rearrange("p s j -> p (s j)"),
-        )
 
         banks = []
-        for h in range(S // HALF):
+        for h in range(2):
             cols = slice(h * HALF, (h + 1) * HALF)
             bank = psum.tile([P, HALF], F32, name=f"bank{h}")
             nc.tensor.matmul_mx(
@@ -75,19 +90,23 @@ def tile_picked_sidegate_silu_l_kernel(tc, xT, side, w1, offs, out):
                 stop=True,
             )
             banks.append(bank)
+        y_first = keep.tile([P, PIECE], F32, name="y_first")
+        nc.scalar.copy(out=y_first[:], in_=banks[0][:, :PIECE])
 
         picked = []
-        for h in range(S // HALF):
+        for h in range(2):
             g = keep.tile([P, HALF], F32, name=f"picked{h}")
-            lo = h * HALF // GROUP
-            nc.vector.tensor_copy(g[:], side_rows[:].indirect(offsets[:, lo : lo + HALF // GROUP]))
+            nc.vector.tensor_copy(g[:], side_rows[:].indirect(halves[h]))
             picked.append(g)
 
-        for lo, hi in PIECES:
+        for lo in range(0, S, PIECE):
             h = lo // HALF
-            cols = slice(lo - h * HALF, hi - h * HALF)
-            gate = keep.tile([P, hi - lo], F32, name=f"gate{lo}")
+            cols = slice(lo - h * HALF, lo - h * HALF + PIECE)
+            gate = keep.tile([P, PIECE], F32, name=f"gate{lo}")
             nc.scalar.activation(gate[:], picked[h][:, cols], SILU)
-            res = keep.tile([P, hi - lo], F32, name=f"res{lo}")
-            nc.vector.tensor_tensor(res[:], banks[h][:, cols], gate[:], MULT)
-            nc.sync.dma_start(out=out[:, lo:hi], in_=res[:])
+            res = keep.tile([P, PIECE], F32, name=f"res{lo}")
+            if lo == 0:
+                nc.gpsimd.tensor_tensor(res[:], y_first[:], gate[:], MULT)
+            else:
+                nc.vector.tensor_tensor(res[:], banks[h][:, cols], gate[:], MULT)
+            nc.sync.dma_start(out=out[:, lo : lo + PIECE], in_=res[:])

@@ -29,14 +29,15 @@ def tile_picked_sidegate_silu_l_kernel(tc, xT, side, w1, offs, out):
 
         offsets = keep.tile([P, S // GROUP], U16, name="offsets")
         x_rows = xT.rearrange("(p j) t -> p j t", j=PACK)
-        planes = [keep.tile([P, T], F32, name=f"plane{j}") for j in range(PACK)]
+        early_planes = keep.tile([P, 2, T], F32, name="early_planes")
+        late_planes = [keep.tile([P, T], F32, name=f"late_plane{j}") for j in range(2)]
         w_raw = keep.tile([P, PACK, N], F32, name="w_raw")
         side_rows = keep.tile([P, T], F32, name="side_rows")
 
-        nc.sync.dma_start(out=planes[0][:], in_=x_rows[:, 0, :])
+        nc.sync.dma_start(out=early_planes[:], in_=x_rows[:, 0:2, :])
         nc.sync.dma_start(offsets[:], offs)
-        for j in range(1, PACK):
-            nc.sync.dma_start(out=planes[j][:], in_=x_rows[:, j, :])
+        for j in range(2):
+            nc.sync.dma_start(out=late_planes[j][:], in_=x_rows[:, 2 + j, :])
         nc.sync.dma_start(out=w_raw[:], in_=w1.rearrange("(p j) m -> p j m", j=PACK))
         nc.sync.dma_start(out=side_rows[:], in_=side)
 
@@ -48,12 +49,15 @@ def tile_picked_sidegate_silu_l_kernel(tc, xT, side, w1, offs, out):
         halves = [offsets[:, h * HALF // GROUP : (h + 1) * HALF // GROUP] for h in range(2)]
         grouped = [keep.tile([P, HALF, PACK], BF16, name=f"grouped{h}", align_bytes=64) for h in range(2)]
         late_pair = keep.tile([P, 2, HALF], F32, name="late_pair")
-        for j in range(PACK):
-            if j < 2:
-                nc.vector.tensor_copy(grouped[1][:, :, j], planes[j][:].indirect(halves[1]))
-            else:
-                nc.vector.tensor_copy(late_pair[:, j - 2, :], planes[j][:].indirect(halves[1]))
-            nc.vector.tensor_copy(grouped[0][:, :, j], planes[j][:].indirect(halves[0]))
+        early_pair = keep.tile([P, 2, S], F32, name="early_pair")
+        for j in range(2):
+            nc.vector.tensor_copy(early_pair[:, j, :], early_planes[:, j, :].indirect(offsets[:]))
+        for h in range(2):
+            cols = slice(h * HALF, (h + 1) * HALF)
+            nc.scalar.copy(out=grouped[h][:, :, 0:2], in_=early_pair[:, :, cols].rearrange("p j s -> p s j"))
+        for j in range(2):
+            nc.vector.tensor_copy(late_pair[:, j, :], late_planes[j][:].indirect(halves[1]))
+            nc.vector.tensor_copy(grouped[0][:, :, 2 + j], late_planes[j][:].indirect(halves[0]))
 
         nc.scalar.copy(out=grouped[1][:, :, 2:4], in_=late_pair[:].rearrange("p j s -> p s j"))
         w_grouped = keep.tile([P, N, PACK], BF16, name="w_grouped", align_bytes=64)

@@ -13,12 +13,14 @@ U8 = mybir.dt.uint8
 FP8X4 = mybir.dt.float8_e4m3fn_x4
 SILU = mybir.ActivationFunctionType.Silu
 MULT = mybir.AluOpType.mult
+ADD = mybir.AluOpType.add
 
 P = 128
 PACK = 4
 GROUP = 16
 HALF = 512
 PIECE = 256
+SIDE_CHUNKS = (1152, 1088, 960, 896)
 
 
 def tile_picked_sidegate_silu_l_kernel(tc, xT, side, w1, offs, out):
@@ -39,12 +41,18 @@ def tile_picked_sidegate_silu_l_kernel(tc, xT, side, w1, offs, out):
         for j in range(2):
             nc.sync.dma_start(out=late_planes[j][:], in_=x_rows[:, 2 + j, :])
         nc.sync.dma_start(out=w_raw[:], in_=w1.rearrange("(p j) m -> p j m", j=PACK))
-        nc.sync.dma_start(out=side_rows[:], in_=side)
+        chunks = []
+        first = 0
+        for width in SIDE_CHUNKS:
+            chunks.append(slice(first, first + width))
+            first = first + width
+        for cols in chunks:
+            nc.sync.dma_start(out=side_rows[:, cols], in_=side[:, cols])
 
-        warm_in = keep.tile([P, 1], F32, name="warm_in")
-        nc.vector.memset(warm_in[:], 0.0)
+        zero = keep.tile([P, 1], F32, name="zero", tag="zero_then_y")
+        nc.vector.memset(zero[:], 0.0)
         warm_out = keep.tile([P, 1], F32, name="warm_out")
-        nc.scalar.activation(warm_out[:], warm_in[:], SILU)
+        nc.scalar.activation(warm_out[:], zero[:], SILU)
 
         halves = [offsets[:, h * HALF // GROUP : (h + 1) * HALF // GROUP] for h in range(2)]
         grouped = [keep.tile([P, HALF, PACK], BF16, name=f"grouped{h}", align_bytes=64) for h in range(2)]
@@ -59,7 +67,9 @@ def tile_picked_sidegate_silu_l_kernel(tc, xT, side, w1, offs, out):
             nc.vector.tensor_copy(late_pair[:, j, :], late_planes[j][:].indirect(halves[1]))
             nc.vector.tensor_copy(grouped[0][:, :, 2 + j], late_planes[j][:].indirect(halves[0]))
 
-        nc.scalar.copy(out=grouped[1][:, :, 2:4], in_=late_pair[:].rearrange("p j s -> p s j"))
+        nc.gpsimd.tensor_scalar(
+            grouped[1][:, :, 2:4], late_pair[:].rearrange("p j s -> p s j"), 1.0, 0.0, op0=MULT, op1=ADD
+        )
         w_grouped = keep.tile([P, N, PACK], BF16, name="w_grouped", align_bytes=64)
         nc.scalar.copy(out=w_grouped[:], in_=w_raw[:].rearrange("p j m -> p m j"))
 
@@ -81,9 +91,9 @@ def tile_picked_sidegate_silu_l_kernel(tc, xT, side, w1, offs, out):
         )
 
         banks = []
-        for h in range(2):
-            cols = slice(h * HALF, (h + 1) * HALF)
-            bank = psum.tile([P, HALF], F32, name=f"bank{h}")
+        for lo, width in ((0, PIECE), (PIECE, PIECE), (HALF, HALF)):
+            cols = slice(lo, lo + width)
+            bank = psum.tile([P, width], F32, name=f"bank{lo}")
             nc.tensor.matmul_mx(
                 out=bank[:],
                 lhsT=w_codes[:].bitcast(FP8X4),
@@ -94,23 +104,29 @@ def tile_picked_sidegate_silu_l_kernel(tc, xT, side, w1, offs, out):
                 stop=True,
             )
             banks.append(bank)
+
+        gate_rows = keep.tile([P, T], F32, name="gate_rows")
+        for cols in chunks:
+            nc.scalar.activation(gate_rows[:, cols], side_rows[:, cols], SILU, bias=zero[:])
+
         y_first = keep.tile([P, PIECE], F32, name="y_first")
-        nc.scalar.copy(out=y_first[:], in_=banks[0][:, :PIECE])
+        nc.vector.tensor_copy(y_first[:], banks[0][:])
+        y_second = keep.tile([P, PIECE], F32, name="y_second", tag="zero_then_y")
+        nc.scalar.copy(out=y_second[:], in_=banks[1][:])
 
-        picked = []
-        for h in range(2):
-            g = keep.tile([P, HALF], F32, name=f"picked{h}")
-            nc.vector.tensor_copy(g[:], side_rows[:].indirect(halves[h]))
-            picked.append(g)
+        picked = keep.tile([P, HALF], F32, name="picked")
+        nc.vector.tensor_copy(picked[:], side_rows[:].indirect(halves[1]))
 
-        for lo in range(0, S, PIECE):
-            h = lo // HALF
-            cols = slice(lo - h * HALF, lo - h * HALF + PIECE)
-            gate = keep.tile([P, PIECE], F32, name=f"gate{lo}")
-            nc.scalar.activation(gate[:], picked[h][:, cols], SILU)
+        for i, y in enumerate((y_first, y_second)):
+            lo = i * PIECE
             res = keep.tile([P, PIECE], F32, name=f"res{lo}")
-            if lo == 0:
-                nc.gpsimd.tensor_tensor(res[:], y_first[:], gate[:], MULT)
-            else:
-                nc.vector.tensor_tensor(res[:], banks[h][:, cols], gate[:], MULT)
+            piece = offsets[:, lo // GROUP : (lo + PIECE) // GROUP]
+            nc.vector.tensor_tensor(res[:], gate_rows[:].indirect(piece), y[:], MULT)
+            nc.sync.dma_start(out=out[:, lo : lo + PIECE], in_=res[:])
+        for lo in range(HALF, S, PIECE):
+            cols = slice(lo - HALF, lo - HALF + PIECE)
+            gate = keep.tile([P, PIECE], F32, name=f"gate{lo}")
+            nc.scalar.activation(gate[:], picked[:, cols], SILU)
+            res = keep.tile([P, PIECE], F32, name=f"res{lo}")
+            nc.vector.tensor_tensor(res[:], banks[2][:, cols], gate[:], MULT)
             nc.sync.dma_start(out=out[:, lo : lo + PIECE], in_=res[:])

@@ -20,7 +20,7 @@ PACK = 4
 GROUP = 16
 HALF = 512
 PIECE = 256
-SIDE_CHUNKS = (1152, 1088, 960, 896)
+SIDE_CHUNKS = (512,) * 8
 
 
 def tile_picked_sidegate_silu_l_kernel(tc, xT, side, w1, offs, out):
@@ -109,19 +109,17 @@ def tile_picked_sidegate_silu_l_kernel(tc, xT, side, w1, offs, out):
         for cols in chunks:
             nc.scalar.activation(gate_rows[:, cols], side_rows[:, cols], SILU, bias=zero[:])
 
-        y_first = keep.tile([P, PIECE], F32, name="y_first")
-        nc.vector.tensor_copy(y_first[:], banks[0][:])
-        y_second = keep.tile([P, PIECE], F32, name="y_second", tag="zero_then_y")
-        nc.scalar.copy(out=y_second[:], in_=banks[1][:])
+        y = keep.tile([P, HALF], F32, name="y", tag="zero_then_y")
+        for i in range(2):
+            nc.scalar.copy(out=y[:, i * PIECE : (i + 1) * PIECE], in_=banks[i][:])
 
         picked = keep.tile([P, HALF], F32, name="picked")
         nc.vector.tensor_copy(picked[:], side_rows[:].indirect(halves[1]))
 
-        for i, y in enumerate((y_first, y_second)):
-            lo = i * PIECE
+        for lo in range(0, HALF, PIECE):
             res = keep.tile([P, PIECE], F32, name=f"res{lo}")
             piece = offsets[:, lo // GROUP : (lo + PIECE) // GROUP]
-            nc.vector.tensor_tensor(res[:], gate_rows[:].indirect(piece), y[:], MULT)
+            nc.vector.tensor_tensor(res[:], gate_rows[:].indirect(piece), y[:, lo : lo + PIECE], MULT)
             nc.sync.dma_start(out=out[:, lo : lo + PIECE], in_=res[:])
         for lo in range(HALF, S, PIECE):
             cols = slice(lo - HALF, lo - HALF + PIECE)

@@ -106,8 +106,9 @@ def tile_picked_sidegate_silu_l_kernel(tc, xT, side, w1, offs, out):
             banks.append(bank)
 
         gate_rows = keep.tile([P, T], F32, name="gate_rows")
-        for cols in chunks:
+        for cols in chunks[:-1]:
             nc.scalar.activation(gate_rows[:, cols], side_rows[:, cols], SILU, bias=zero[:])
+        nc.scalar.activation(gate_rows[:, chunks[-1]], side_rows[:, chunks[-1]], SILU)
 
         y = keep.tile([P, HALF], F32, name="y", tag="zero_then_y")
         for i in range(2):

@@ -20,7 +20,7 @@ PACK = 4
 GROUP = 16
 HALF = 512
 PIECE = 256
-SIDE_CHUNKS = (512,) * 8
+SIDE_CHUNKS = (736, 704, 704, 672, 640, 640)
 
 
 def tile_picked_sidegate_silu_l_kernel(tc, xT, side, w1, offs, out):
@@ -91,7 +91,7 @@ def tile_picked_sidegate_silu_l_kernel(tc, xT, side, w1, offs, out):
         )
 
         banks = []
-        for lo, width in ((0, PIECE), (PIECE, PIECE), (HALF, HALF)):
+        for lo, width in ((0, HALF), (HALF, HALF)):
             cols = slice(lo, lo + width)
             bank = psum.tile([P, width], F32, name=f"bank{lo}")
             nc.tensor.matmul_mx(
@@ -111,21 +111,25 @@ def tile_picked_sidegate_silu_l_kernel(tc, xT, side, w1, offs, out):
         nc.scalar.activation(gate_rows[:, chunks[-1]], side_rows[:, chunks[-1]], SILU)
 
         y = keep.tile([P, HALF], F32, name="y", tag="zero_then_y")
-        for i in range(2):
-            nc.scalar.copy(out=y[:, i * PIECE : (i + 1) * PIECE], in_=banks[i][:])
+        nc.scalar.copy(out=y[:, :192], in_=banks[0][:, :192])
+        nc.scalar.copy(out=y[:, 192:], in_=banks[0][:, 192:])
 
         picked = keep.tile([P, HALF], F32, name="picked")
         nc.vector.tensor_copy(picked[:], side_rows[:].indirect(halves[1]))
 
-        for lo in range(0, HALF, PIECE):
-            res = keep.tile([P, PIECE], F32, name=f"res{lo}")
-            piece = offsets[:, lo // GROUP : (lo + PIECE) // GROUP]
-            nc.vector.tensor_tensor(res[:], gate_rows[:].indirect(piece), y[:, lo : lo + PIECE], MULT)
-            nc.sync.dma_start(out=out[:, lo : lo + PIECE], in_=res[:])
+        def fused_piece(lo, hi, tag):
+            res = keep.tile([P, hi - lo], F32, name=f"res{lo}", tag=tag)
+            piece = offsets[:, lo // GROUP : hi // GROUP]
+            nc.vector.tensor_tensor(res[:], gate_rows[:].indirect(piece), y[:, lo:hi], MULT)
+            nc.sync.dma_start(out=out[:, lo:hi], in_=res[:])
+
+        fused_piece(0, 192, "res0")
+        fused_piece(192, 384, "res192")
         for lo in range(HALF, S, PIECE):
             cols = slice(lo - HALF, lo - HALF + PIECE)
-            gate = keep.tile([P, PIECE], F32, name=f"gate{lo}")
+            gate = keep.tile([P, PIECE], F32, name=f"gate{lo}", tag=f"gate{lo}")
             nc.scalar.activation(gate[:], picked[:, cols], SILU)
             res = keep.tile([P, PIECE], F32, name=f"res{lo}")
-            nc.vector.tensor_tensor(res[:], banks[2][:, cols], gate[:], MULT)
+            nc.vector.tensor_tensor(res[:], banks[1][:, cols], gate[:], MULT)
             nc.sync.dma_start(out=out[:, lo : lo + PIECE], in_=res[:])
+        fused_piece(384, HALF, f"gate{HALF}")

@@ -20,7 +20,7 @@ PACK = 4
 GROUP = 16
 HALF = 512
 PIECE = 256
-SIDE_CHUNKS = (736, 704, 704, 672, 640, 640)
+SIDE_CHUNKS = (960, 896, 800, 768, 672)
 
 
 def tile_picked_sidegate_silu_l_kernel(tc, xT, side, w1, offs, out):
@@ -31,13 +31,14 @@ def tile_picked_sidegate_silu_l_kernel(tc, xT, side, w1, offs, out):
 
         offsets = keep.tile([P, S // GROUP], U16, name="offsets")
         x_rows = xT.rearrange("(p j) t -> p j t", j=PACK)
-        early_planes = keep.tile([P, 2, T], F32, name="early_planes")
+        early_planes = [keep.tile([P, T], F32, name=f"early_plane{j}") for j in range(2)]
         late_planes = [keep.tile([P, T], F32, name=f"late_plane{j}") for j in range(2)]
         w_raw = keep.tile([P, PACK, N], F32, name="w_raw")
         side_rows = keep.tile([P, T], F32, name="side_rows")
 
-        nc.sync.dma_start(out=early_planes[:], in_=x_rows[:, 0:2, :])
+        nc.scalar.dma_start(out=early_planes[0][:], in_=x_rows[:, 0, :])
         nc.sync.dma_start(offsets[:], offs)
+        nc.sync.dma_start(out=early_planes[1][:], in_=x_rows[:, 1, :])
         for j in range(2):
             nc.sync.dma_start(out=late_planes[j][:], in_=x_rows[:, 2 + j, :])
         nc.sync.dma_start(out=w_raw[:], in_=w1.rearrange("(p j) m -> p j m", j=PACK))
@@ -59,7 +60,7 @@ def tile_picked_sidegate_silu_l_kernel(tc, xT, side, w1, offs, out):
         late_pair = keep.tile([P, 2, HALF], F32, name="late_pair")
         early_pair = keep.tile([P, 2, S], F32, name="early_pair")
         for j in range(2):
-            nc.vector.tensor_copy(early_pair[:, j, :], early_planes[:, j, :].indirect(offsets[:]))
+            nc.vector.tensor_copy(early_pair[:, j, :], early_planes[j][:].indirect(offsets[:]))
         for h in range(2):
             cols = slice(h * HALF, (h + 1) * HALF)
             nc.scalar.copy(out=grouped[h][:, :, 0:2], in_=early_pair[:, :, cols].rearrange("p j s -> p s j"))
@@ -124,7 +125,7 @@ def tile_picked_sidegate_silu_l_kernel(tc, xT, side, w1, offs, out):
             nc.sync.dma_start(out=out[:, lo:hi], in_=res[:])
 
         fused_piece(0, 192, "res0")
-        fused_piece(192, 384, "res192")
+        fused_piece(192, 352, "res192")
         for lo in range(HALF, S, PIECE):
             cols = slice(lo - HALF, lo - HALF + PIECE)
             gate = keep.tile([P, PIECE], F32, name=f"gate{lo}", tag=f"gate{lo}")
@@ -132,4 +133,4 @@ def tile_picked_sidegate_silu_l_kernel(tc, xT, side, w1, offs, out):
             res = keep.tile([P, PIECE], F32, name=f"res{lo}")
             nc.vector.tensor_tensor(res[:], banks[1][:, cols], gate[:], MULT)
             nc.sync.dma_start(out=out[:, lo : lo + PIECE], in_=res[:])
-        fused_piece(384, HALF, f"gate{HALF}")
+        fused_piece(352, HALF, f"gate{HALF}")

@@ -20,7 +20,7 @@ PACK = 4
 GROUP = 16
 HALF = 512
 PIECE = 256
-SIDE_CHUNKS = (960, 896, 800, 768, 672)
+SIDE_CHUNKS = (896, 864, 800, 768, 768)
 
 
 def tile_picked_sidegate_silu_l_kernel(tc, xT, side, w1, offs, out):
@@ -112,8 +112,8 @@ def tile_picked_sidegate_silu_l_kernel(tc, xT, side, w1, offs, out):
         nc.scalar.activation(gate_rows[:, chunks[-1]], side_rows[:, chunks[-1]], SILU)
 
         y = keep.tile([P, HALF], F32, name="y", tag="zero_then_y")
-        nc.scalar.copy(out=y[:, :192], in_=banks[0][:, :192])
-        nc.scalar.copy(out=y[:, 192:], in_=banks[0][:, 192:])
+        nc.scalar.copy(out=y[:, :160], in_=banks[0][:, :160])
+        nc.scalar.copy(out=y[:, 160:], in_=banks[0][:, 160:])
 
         picked = keep.tile([P, HALF], F32, name="picked")
         nc.vector.tensor_copy(picked[:], side_rows[:].indirect(halves[1]))
@@ -124,8 +124,8 @@ def tile_picked_sidegate_silu_l_kernel(tc, xT, side, w1, offs, out):
             nc.vector.tensor_tensor(res[:], gate_rows[:].indirect(piece), y[:, lo:hi], MULT)
             nc.sync.dma_start(out=out[:, lo:hi], in_=res[:])
 
-        fused_piece(0, 192, "res0")
-        fused_piece(192, 352, "res192")
+        fused_piece(0, 160, "res0")
+        fused_piece(160, 384, "res160")
         for lo in range(HALF, S, PIECE):
             cols = slice(lo - HALF, lo - HALF + PIECE)
             gate = keep.tile([P, PIECE], F32, name=f"gate{lo}", tag=f"gate{lo}")
@@ -133,4 +133,4 @@ def tile_picked_sidegate_silu_l_kernel(tc, xT, side, w1, offs, out):
             res = keep.tile([P, PIECE], F32, name=f"res{lo}")
             nc.vector.tensor_tensor(res[:], banks[1][:, cols], gate[:], MULT)
             nc.sync.dma_start(out=out[:, lo : lo + PIECE], in_=res[:])
-        fused_piece(352, HALF, f"gate{HALF}")
+        fused_piece(384, HALF, f"gate{HALF}")

@@ -20,7 +20,7 @@ PACK = 4
 GROUP = 16
 HALF = 512
 PIECE = 256
-SIDE_CHUNKS = (896, 864, 800, 768, 768)
+SIDE_CHUNKS = (896, 832, 832, 768, 768)
 
 
 def tile_picked_sidegate_silu_l_kernel(tc, xT, side, w1, offs, out):
@@ -31,10 +31,10 @@ def tile_picked_sidegate_silu_l_kernel(tc, xT, side, w1, offs, out):
 
         offsets = keep.tile([P, S // GROUP], U16, name="offsets")
         x_rows = xT.rearrange("(p j) t -> p j t", j=PACK)
-        early_planes = [keep.tile([P, T], F32, name=f"early_plane{j}") for j in range(2)]
-        late_planes = [keep.tile([P, T], F32, name=f"late_plane{j}") for j in range(2)]
-        w_raw = keep.tile([P, PACK, N], F32, name="w_raw")
-        side_rows = keep.tile([P, T], F32, name="side_rows")
+        early_planes = [keep.tile([P, T], F32, name=f"early_plane{j}", align_bytes=256) for j in range(2)]
+        late_planes = [keep.tile([P, T], F32, name=f"late_plane{j}", align_bytes=256) for j in range(2)]
+        w_raw = keep.tile([P, PACK, N], F32, name="w_raw", align_bytes=256)
+        side_rows = keep.tile([P, T], F32, name="side_rows", align_bytes=256)
 
         nc.scalar.dma_start(out=early_planes[0][:], in_=x_rows[:, 0, :])
         nc.sync.dma_start(offsets[:], offs)

@@ -12,6 +12,7 @@ U16 = mybir.dt.uint16
 U8 = mybir.dt.uint8
 FP8X4 = mybir.dt.float8_e4m3fn_x4
 SILU = mybir.ActivationFunctionType.Silu
+IDENTITY = mybir.ActivationFunctionType.Identity
 MULT = mybir.AluOpType.mult
 ADD = mybir.AluOpType.add
 
@@ -37,8 +38,8 @@ def tile_picked_sidegate_silu_l_kernel(tc, xT, side, w1, offs, out):
         side_rows = keep.tile([P, T], F32, name="side_rows", align_bytes=256)
 
         nc.scalar.dma_start(out=early_planes[0][:], in_=x_rows[:, 0, :])
-        nc.sync.dma_start(offsets[:], offs)
         nc.sync.dma_start(out=early_planes[1][:], in_=x_rows[:, 1, :])
+        nc.sync.dma_start(offsets[:], offs)
         for j in range(2):
             nc.sync.dma_start(out=late_planes[j][:], in_=x_rows[:, 2 + j, :])
         nc.sync.dma_start(out=w_raw[:], in_=w1.rearrange("(p j) m -> p j m", j=PACK))
@@ -63,7 +64,9 @@ def tile_picked_sidegate_silu_l_kernel(tc, xT, side, w1, offs, out):
             nc.vector.tensor_copy(early_pair[:, j, :], early_planes[j][:].indirect(offsets[:]))
         for h in range(2):
             cols = slice(h * HALF, (h + 1) * HALF)
-            nc.scalar.copy(out=grouped[h][:, :, 0:2], in_=early_pair[:, :, cols].rearrange("p j s -> p s j"))
+            nc.scalar.activation(
+                grouped[h][:, :, 0:2], early_pair[:, :, cols].rearrange("p j s -> p s j"), IDENTITY, bias=warm_out[:]
+            )
         for j in range(2):
             nc.vector.tensor_copy(late_pair[:, j, :], late_planes[j][:].indirect(halves[1]))
             nc.vector.tensor_copy(grouped[0][:, :, 2 + j], late_planes[j][:].indirect(halves[0]))

@@ -21,7 +21,7 @@ PACK = 4
 GROUP = 16
 HALF = 512
 PIECE = 256
-SIDE_CHUNKS = (896, 832, 832, 768, 768)
+SIDE_CHUNKS = (1024, 1024, 1024, 1024)
 
 
 def tile_picked_sidegate_silu_l_kernel(tc, xT, side, w1, offs, out):
@@ -58,7 +58,7 @@ def tile_picked_sidegate_silu_l_kernel(tc, xT, side, w1, offs, out):
 
         halves = [offsets[:, h * HALF // GROUP : (h + 1) * HALF // GROUP] for h in range(2)]
         grouped = [keep.tile([P, HALF, PACK], BF16, name=f"grouped{h}", align_bytes=64) for h in range(2)]
-        late_pair = keep.tile([P, 2, HALF], F32, name="late_pair")
+        late_pair = keep.tile([P, 2, HALF], F32, name="late_pair", tag="pair_then_y")
         early_pair = keep.tile([P, 2, S], F32, name="early_pair")
         for j in range(2):
             nc.vector.tensor_copy(early_pair[:, j, :], early_planes[j][:].indirect(offsets[:]))
@@ -77,63 +77,60 @@ def tile_picked_sidegate_silu_l_kernel(tc, xT, side, w1, offs, out):
         w_grouped = keep.tile([P, N, PACK], BF16, name="w_grouped", align_bytes=64)
         nc.scalar.copy(out=w_grouped[:], in_=w_raw[:].rearrange("p j m -> p m j"))
 
-        x_codes = keep.tile([P, S], U32, name="x_codes", align_bytes=64)
-        x_scales = keep.tile([P, S], U8, name="x_scales", align_bytes=64)
-        for h in range(2):
-            cols = slice(h * HALF, (h + 1) * HALF)
+        def quantize(source, width, name):
+            codes = keep.tile([P, width], U32, name=f"{name}_codes", align_bytes=64)
+            scales = keep.tile([P, width], U8, name=f"{name}_scales", align_bytes=64)
             nc.vector.quantize_mx(
-                out=x_codes[:, cols].bitcast(FP8X4),
-                scales=x_scales[:, cols],
-                in_=grouped[h][:].rearrange("p s j -> p (s j)"),
+                out=codes[:].bitcast(FP8X4), scales=scales[:], in_=source.rearrange("p c j -> p (c j)")
             )
-        w_codes = keep.tile([P, N], U32, name="w_codes", align_bytes=64)
-        w_scales = keep.tile([P, N], U8, name="w_scales", align_bytes=64)
-        nc.vector.quantize_mx(
-            out=w_codes[:].bitcast(FP8X4),
-            scales=w_scales[:],
-            in_=w_grouped[:].rearrange("p m j -> p (m j)"),
-        )
+            return codes, scales
+
+        quarter0 = quantize(grouped[0][:, :PIECE, :], PIECE, "x0")
+        w_codes, w_scales = quantize(w_grouped[:], N, "w")
+        quarter1 = quantize(grouped[0][:, PIECE:, :], PIECE, "x1")
+        half1 = quantize(grouped[1][:], HALF, "x2")
 
         banks = []
-        for lo, width in ((0, HALF), (HALF, HALF)):
-            cols = slice(lo, lo + width)
-            bank = psum.tile([P, width], F32, name=f"bank{lo}")
+        for b, (x_codes, x_scales) in enumerate((quarter0, quarter1, half1)):
+            bank = psum.tile([P, x_codes.shape[1]], F32, name=f"bank{b}")
             nc.tensor.matmul_mx(
                 out=bank[:],
                 lhsT=w_codes[:].bitcast(FP8X4),
                 lhsT_scale=w_scales[:],
-                rhs=x_codes[:, cols].bitcast(FP8X4),
-                rhs_scale=x_scales[:, cols],
+                rhs=x_codes[:].bitcast(FP8X4),
+                rhs_scale=x_scales[:],
                 start=True,
                 stop=True,
             )
             banks.append(bank)
+        y_first = keep.tile([P, 160], F32, name="y_first", tag="pair_then_y")
+        nc.vector.tensor_copy(y_first[:], banks[0][:, :160])
 
         gate_rows = keep.tile([P, T], F32, name="gate_rows")
         for cols in chunks[:-1]:
             nc.scalar.activation(gate_rows[:, cols], side_rows[:, cols], SILU, bias=zero[:])
         nc.scalar.activation(gate_rows[:, chunks[-1]], side_rows[:, chunks[-1]], SILU)
 
-        y = keep.tile([P, HALF], F32, name="y", tag="zero_then_y")
-        nc.scalar.copy(out=y[:, :160], in_=banks[0][:, :160])
-        nc.scalar.copy(out=y[:, 160:], in_=banks[0][:, 160:])
+        y_second = keep.tile([P, 352], F32, name="y_second", tag="zero_then_y")
+        nc.scalar.copy(out=y_second[:, :96], in_=banks[0][:, 160:])
+        nc.scalar.copy(out=y_second[:, 96:], in_=banks[1][:])
 
         picked = keep.tile([P, HALF], F32, name="picked")
         nc.vector.tensor_copy(picked[:], side_rows[:].indirect(halves[1]))
 
-        def fused_piece(lo, hi, tag):
+        def fused_piece(lo, hi, y, tag):
             res = keep.tile([P, hi - lo], F32, name=f"res{lo}", tag=tag)
             piece = offsets[:, lo // GROUP : hi // GROUP]
-            nc.vector.tensor_tensor(res[:], gate_rows[:].indirect(piece), y[:, lo:hi], MULT)
+            nc.vector.tensor_tensor(res[:], gate_rows[:].indirect(piece), y, MULT)
             nc.sync.dma_start(out=out[:, lo:hi], in_=res[:])
 
-        fused_piece(0, 160, "res0")
-        fused_piece(160, 384, "res160")
+        fused_piece(0, 160, y_first[:], "res0")
+        fused_piece(160, 384, y_second[:, :224], "res160")
         for lo in range(HALF, S, PIECE):
             cols = slice(lo - HALF, lo - HALF + PIECE)
             gate = keep.tile([P, PIECE], F32, name=f"gate{lo}", tag=f"gate{lo}")
             nc.scalar.activation(gate[:], picked[:, cols], SILU)
             res = keep.tile([P, PIECE], F32, name=f"res{lo}")
-            nc.vector.tensor_tensor(res[:], banks[1][:, cols], gate[:], MULT)
+            nc.vector.tensor_tensor(res[:], banks[2][:, cols], gate[:], MULT)
             nc.sync.dma_start(out=out[:, lo : lo + PIECE], in_=res[:])
-        fused_piece(384, HALF, f"gate{HALF}")
+        fused_piece(384, HALF, y_second[:, 224:], f"gate{HALF}")

@@ -34,7 +34,7 @@ def tile_picked_sidegate_silu_l_kernel(tc, xT, side, w1, offs, out):
         x_rows = xT.rearrange("(p j) t -> p j t", j=PACK)
         early_planes = [keep.tile([P, T], F32, name=f"early_plane{j}", align_bytes=256) for j in range(2)]
         late_planes = [keep.tile([P, T], F32, name=f"late_plane{j}", align_bytes=256) for j in range(2)]
-        w_raw = keep.tile([P, PACK, N], F32, name="w_raw", align_bytes=256)
+        w_raw = keep.tile([P, PACK, N], F32, name="w_raw", tag="w_then_codes", align_bytes=256)
         side_rows = keep.tile([P, T], F32, name="side_rows", align_bytes=256)
 
         nc.scalar.dma_start(out=early_planes[0][:], in_=x_rows[:, 0, :])
@@ -77,18 +77,18 @@ def tile_picked_sidegate_silu_l_kernel(tc, xT, side, w1, offs, out):
         w_grouped = keep.tile([P, N, PACK], BF16, name="w_grouped", align_bytes=64)
         nc.scalar.copy(out=w_grouped[:], in_=w_raw[:].rearrange("p j m -> p m j"))
 
-        def quantize(source, width, name):
-            codes = keep.tile([P, width], U32, name=f"{name}_codes", align_bytes=64)
+        def quantize(source, width, name, tag):
+            codes = keep.tile([P, width], U32, name=f"{name}_codes", tag=tag, align_bytes=256)
             scales = keep.tile([P, width], U8, name=f"{name}_scales", align_bytes=64)
             nc.vector.quantize_mx(
                 out=codes[:].bitcast(FP8X4), scales=scales[:], in_=source.rearrange("p c j -> p (c j)")
             )
             return codes, scales
 
-        quarter0 = quantize(grouped[0][:, :PIECE, :], PIECE, "x0")
-        w_codes, w_scales = quantize(w_grouped[:], N, "w")
-        quarter1 = quantize(grouped[0][:, PIECE:, :], PIECE, "x1")
-        half1 = quantize(grouped[1][:], HALF, "x2")
+        quarter0 = quantize(grouped[0][:, :PIECE, :], PIECE, "x0", "x0_codes")
+        w_codes, w_scales = quantize(w_grouped[:], N, "w", "w_codes")
+        quarter1 = quantize(grouped[0][:, PIECE:, :], PIECE, "x1", "w_then_codes")
+        half1 = quantize(grouped[1][:], HALF, "x2", "x2_codes")
 
         banks = []
         for b, (x_codes, x_scales) in enumerate((quarter0, quarter1, half1)):

@@ -119,18 +119,18 @@ def tile_picked_sidegate_silu_l_kernel(tc, xT, side, w1, offs, out):
         nc.vector.tensor_copy(picked[:], side_rows[:].indirect(halves[1]))
 
         def fused_piece(lo, hi, y, tag):
-            res = keep.tile([P, hi - lo], F32, name=f"res{lo}", tag=tag)
+            res = keep.tile([P, hi - lo], F32, name=f"res{lo}", tag=tag, align_bytes=256)
             piece = offsets[:, lo // GROUP : hi // GROUP]
             nc.vector.tensor_tensor(res[:], gate_rows[:].indirect(piece), y, MULT)
             nc.sync.dma_start(out=out[:, lo:hi], in_=res[:])
 
         fused_piece(0, 160, y_first[:], "res0")
-        fused_piece(160, 384, y_second[:, :224], "res160")
+        fused_piece(160, 352, y_second[:, :192], "res160")
         for lo in range(HALF, S, PIECE):
             cols = slice(lo - HALF, lo - HALF + PIECE)
-            gate = keep.tile([P, PIECE], F32, name=f"gate{lo}", tag=f"gate{lo}")
+            gate = keep.tile([P, PIECE], F32, name=f"gate{lo}", tag=f"gate{lo}", align_bytes=256)
             nc.scalar.activation(gate[:], picked[:, cols], SILU)
-            res = keep.tile([P, PIECE], F32, name=f"res{lo}")
+            res = keep.tile([P, PIECE], F32, name=f"res{lo}", align_bytes=256)
             nc.vector.tensor_tensor(res[:], banks[2][:, cols], gate[:], MULT)
             nc.sync.dma_start(out=out[:, lo : lo + PIECE], in_=res[:])
-        fused_piece(384, HALF, y_second[:, 224:], f"gate{HALF}")
+        fused_piece(352, HALF, y_second[:, 192:], f"gate{HALF}")

@@ -85,9 +85,9 @@ def tile_picked_sidegate_silu_l_kernel(tc, xT, side, w1, offs, out):
             )
             return codes, scales
 
-        quarter0 = quantize(grouped[0][:, :PIECE, :], PIECE, "x0", "x0_codes")
+        quarter0 = quantize(grouped[0][:, PIECE:, :], PIECE, "x0", "x0_codes")
         w_codes, w_scales = quantize(w_grouped[:], N, "w", "w_codes")
-        quarter1 = quantize(grouped[0][:, PIECE:, :], PIECE, "x1", "w_then_codes")
+        quarter1 = quantize(grouped[0][:, :PIECE, :], PIECE, "x1", "w_then_codes")
         half1 = quantize(grouped[1][:], HALF, "x2", "x2_codes")
 
         banks = []
@@ -104,7 +104,7 @@ def tile_picked_sidegate_silu_l_kernel(tc, xT, side, w1, offs, out):
             )
             banks.append(bank)
         y_first = keep.tile([P, 160], F32, name="y_first", tag="pair_then_y")
-        nc.vector.tensor_copy(y_first[:], banks[0][:, :160])
+        nc.vector.tensor_copy(y_first[:], banks[0][:, 96:])
 
         gate_rows = keep.tile([P, T], F32, name="gate_rows")
         for cols in chunks[:-1]:
@@ -112,8 +112,8 @@ def tile_picked_sidegate_silu_l_kernel(tc, xT, side, w1, offs, out):
         nc.scalar.activation(gate_rows[:, chunks[-1]], side_rows[:, chunks[-1]], SILU)
 
         y_second = keep.tile([P, 352], F32, name="y_second", tag="zero_then_y")
-        nc.scalar.copy(out=y_second[:, :96], in_=banks[0][:, 160:])
-        nc.scalar.copy(out=y_second[:, 96:], in_=banks[1][:])
+        nc.scalar.copy(out=y_second[:, :PIECE], in_=banks[1][:])
+        nc.scalar.copy(out=y_second[:, PIECE:], in_=banks[0][:, :96])
 
         picked = keep.tile([P, HALF], F32, name="picked")
         nc.vector.tensor_copy(picked[:], side_rows[:].indirect(halves[1]))
@@ -124,8 +124,8 @@ def tile_picked_sidegate_silu_l_kernel(tc, xT, side, w1, offs, out):
             nc.vector.tensor_tensor(res[:], gate_rows[:].indirect(piece), y, MULT)
             nc.sync.dma_start(out=out[:, lo:hi], in_=res[:])
 
-        fused_piece(0, 160, y_first[:], "res0")
-        fused_piece(160, 352, y_second[:, :192], "res160")
+        fused_piece(352, HALF, y_first[:], "res352")
+        fused_piece(0, 192, y_second[:, :192], "res0")
         for lo in range(HALF, S, PIECE):
             cols = slice(lo - HALF, lo - HALF + PIECE)
             gate = keep.tile([P, PIECE], F32, name=f"gate{lo}", tag=f"gate{lo}", align_bytes=256)
@@ -133,4 +133,4 @@ def tile_picked_sidegate_silu_l_kernel(tc, xT, side, w1, offs, out):
             res = keep.tile([P, PIECE], F32, name=f"res{lo}", align_bytes=256)
             nc.vector.tensor_tensor(res[:], banks[2][:, cols], gate[:], MULT)
             nc.sync.dma_start(out=out[:, lo : lo + PIECE], in_=res[:])
-        fused_piece(352, HALF, y_second[:, 192:], f"gate{HALF}")
+        fused_piece(192, 352, y_second[:, 192:], f"gate{HALF}")

@@ -21,6 +21,8 @@ PACK = 4
 GROUP = 16
 HALF = 512
 PIECE = 256
+MIDDLE = 192
+LATE = 352
 SIDE_CHUNKS = (1024, 1024, 1024, 1024)
 
 
@@ -103,17 +105,18 @@ def tile_picked_sidegate_silu_l_kernel(tc, xT, side, w1, offs, out):
                 stop=True,
             )
             banks.append(bank)
-        y_first = keep.tile([P, 160], F32, name="y_first", tag="pair_then_y")
-        nc.vector.tensor_copy(y_first[:], banks[0][:, 96:])
+        y_first = keep.tile([P, HALF - LATE], F32, name="y_first", tag="pair_then_y")
+        nc.vector.tensor_copy(y_first[:], banks[0][:, LATE - PIECE :])
 
         gate_rows = keep.tile([P, T], F32, name="gate_rows")
         for cols in chunks[:-1]:
             nc.scalar.activation(gate_rows[:, cols], side_rows[:, cols], SILU, bias=zero[:])
         nc.scalar.activation(gate_rows[:, chunks[-1]], side_rows[:, chunks[-1]], SILU)
 
-        y_second = keep.tile([P, 352], F32, name="y_second", tag="zero_then_y")
-        nc.scalar.copy(out=y_second[:, :PIECE], in_=banks[1][:])
-        nc.scalar.copy(out=y_second[:, PIECE:], in_=banks[0][:, :96])
+        y_second = keep.tile([P, LATE], F32, name="y_second", tag="zero_then_y")
+        nc.scalar.copy(out=y_second[:, PIECE:], in_=banks[0][:, : LATE - PIECE])
+        nc.scalar.copy(out=y_second[:, MIDDLE:PIECE], in_=banks[1][:, MIDDLE:])
+        nc.scalar.copy(out=y_second[:, :MIDDLE], in_=banks[1][:, :MIDDLE])
 
         picked = keep.tile([P, HALF], F32, name="picked")
         nc.vector.tensor_copy(picked[:], side_rows[:].indirect(halves[1]))
@@ -124,8 +127,8 @@ def tile_picked_sidegate_silu_l_kernel(tc, xT, side, w1, offs, out):
             nc.vector.tensor_tensor(res[:], gate_rows[:].indirect(piece), y, MULT)
             nc.sync.dma_start(out=out[:, lo:hi], in_=res[:])
 
-        fused_piece(352, HALF, y_first[:], "res352")
-        fused_piece(0, 192, y_second[:, :192], "res0")
+        fused_piece(LATE, HALF, y_first[:], "res352")
+        fused_piece(MIDDLE, LATE, y_second[:, MIDDLE:], "res192")
         for lo in range(HALF, S, PIECE):
             cols = slice(lo - HALF, lo - HALF + PIECE)
             gate = keep.tile([P, PIECE], F32, name=f"gate{lo}", tag=f"gate{lo}", align_bytes=256)
@@ -133,4 +136,4 @@ def tile_picked_sidegate_silu_l_kernel(tc, xT, side, w1, offs, out):
             res = keep.tile([P, PIECE], F32, name=f"res{lo}", align_bytes=256)
             nc.vector.tensor_tensor(res[:], banks[2][:, cols], gate[:], MULT)
             nc.sync.dma_start(out=out[:, lo : lo + PIECE], in_=res[:])
-        fused_piece(192, 352, y_second[:, 192:], f"gate{HALF}")
+        fused_piece(0, MIDDLE, y_second[:, :MIDDLE], f"gate{HALF}")

@@ -42,8 +42,9 @@ def tile_picked_sidegate_silu_l_kernel(tc, xT, side, w1, offs, out):
         nc.scalar.dma_start(out=early_planes[0][:], in_=x_rows[:, 0, :])
         nc.sync.dma_start(out=early_planes[1][:], in_=x_rows[:, 1, :])
         nc.sync.dma_start(offsets[:], offs)
-        for j in range(2):
-            nc.sync.dma_start(out=late_planes[j][:], in_=x_rows[:, 2 + j, :])
+        nc.scalar.dma_start(out=late_planes[0][:, : T // 2], in_=x_rows[:, 2, : T // 2])
+        nc.sync.dma_start(out=late_planes[0][:, T // 2 :], in_=x_rows[:, 2, T // 2 :])
+        nc.sync.dma_start(out=late_planes[1][:], in_=x_rows[:, 3, :])
         nc.sync.dma_start(out=w_raw[:], in_=w1.rearrange("(p j) m -> p j m", j=PACK))
         chunks = []
         first = 0

@@ -12,18 +12,16 @@ U16 = mybir.dt.uint16
 U8 = mybir.dt.uint8
 FP8X4 = mybir.dt.float8_e4m3fn_x4
 SILU = mybir.ActivationFunctionType.Silu
-IDENTITY = mybir.ActivationFunctionType.Identity
+COPY = mybir.ActivationFunctionType.Copy
 MULT = mybir.AluOpType.mult
-ADD = mybir.AluOpType.add
 
 P = 128
 PACK = 4
 GROUP = 16
-HALF = 512
-PIECE = 256
-MIDDLE = 192
-LATE = 352
-SIDE_CHUNKS = (1024, 1024, 1024, 1024)
+BANK = 512
+X_VECTOR = 768
+VECTOR_PIECES = ((0, 256), (256, 512))
+SCALAR_PIECES = ((512, 768), (768, 896), (896, 1024))
 
 
 def tile_picked_sidegate_silu_l_kernel(tc, xT, side, w1, offs, out):
@@ -34,70 +32,50 @@ def tile_picked_sidegate_silu_l_kernel(tc, xT, side, w1, offs, out):
 
         offsets = keep.tile([P, S // GROUP], U16, name="offsets")
         x_rows = xT.rearrange("(p j) t -> p j t", j=PACK)
-        early_planes = [keep.tile([P, T], F32, name=f"early_plane{j}", align_bytes=256) for j in range(2)]
-        late_planes = [keep.tile([P, T], F32, name=f"late_plane{j}", align_bytes=256) for j in range(2)]
-        w_raw = keep.tile([P, PACK, N], F32, name="w_raw", tag="w_then_codes", align_bytes=256)
+        planes = [keep.tile([P, T], F32, name=f"plane{j}", align_bytes=256) for j in range(PACK)]
+        w_raw = keep.tile([P, PACK, N], F32, name="w_raw", align_bytes=256)
         side_rows = keep.tile([P, T], F32, name="side_rows", align_bytes=256)
 
-        nc.scalar.dma_start(out=early_planes[0][:], in_=x_rows[:, 0, :])
-        nc.sync.dma_start(out=early_planes[1][:], in_=x_rows[:, 1, :])
+        nc.scalar.dma_start(out=planes[0][:], in_=x_rows[:, 0, :])
+        nc.sync.dma_start(out=planes[1][:], in_=x_rows[:, 1, :])
         nc.sync.dma_start(offsets[:], offs)
-        nc.scalar.dma_start(out=late_planes[0][:, : T // 2], in_=x_rows[:, 2, : T // 2])
-        nc.sync.dma_start(out=late_planes[0][:, T // 2 :], in_=x_rows[:, 2, T // 2 :])
-        nc.sync.dma_start(out=late_planes[1][:], in_=x_rows[:, 3, :])
+        nc.scalar.dma_start(out=planes[2][:, : T // 2], in_=x_rows[:, 2, : T // 2])
+        nc.sync.dma_start(out=planes[2][:, T // 2 :], in_=x_rows[:, 2, T // 2 :])
+        nc.sync.dma_start(out=planes[3][:], in_=x_rows[:, 3, :])
         nc.sync.dma_start(out=w_raw[:], in_=w1.rearrange("(p j) m -> p j m", j=PACK))
-        chunks = []
-        first = 0
-        for width in SIDE_CHUNKS:
-            chunks.append(slice(first, first + width))
-            first = first + width
-        for cols in chunks:
-            nc.sync.dma_start(out=side_rows[:, cols], in_=side[:, cols])
+        nc.sync.dma_start(out=side_rows[:], in_=side)
 
-        zero = keep.tile([P, 1], F32, name="zero", tag="zero_then_y")
+        zero = keep.tile([P, 1], F32, name="zero")
         nc.vector.memset(zero[:], 0.0)
         warm_out = keep.tile([P, 1], F32, name="warm_out")
         nc.scalar.activation(warm_out[:], zero[:], SILU)
 
-        halves = [offsets[:, h * HALF // GROUP : (h + 1) * HALF // GROUP] for h in range(2)]
-        grouped = [keep.tile([P, HALF, PACK], BF16, name=f"grouped{h}", align_bytes=64) for h in range(2)]
-        late_pair = keep.tile([P, 2, HALF], F32, name="late_pair", tag="pair_then_y")
-        early_pair = keep.tile([P, 2, S], F32, name="early_pair")
-        for j in range(2):
-            nc.vector.tensor_copy(early_pair[:, j, :], early_planes[j][:].indirect(offsets[:]))
-        for h in range(2):
-            cols = slice(h * HALF, (h + 1) * HALF)
-            nc.scalar.activation(
-                grouped[h][:, :, 0:2], early_pair[:, :, cols].rearrange("p j s -> p s j"), IDENTITY, bias=warm_out[:]
-            )
-        for j in range(2):
-            nc.vector.tensor_copy(late_pair[:, j, :], late_planes[j][:].indirect(halves[1]))
-            nc.vector.tensor_copy(grouped[0][:, :, 2 + j], late_planes[j][:].indirect(halves[0]))
+        def entries(lo, hi):
+            return offsets[:, lo // GROUP : hi // GROUP]
 
-        nc.gpsimd.tensor_scalar(
-            grouped[1][:, :, 2:4], late_pair[:].rearrange("p j s -> p s j"), 1.0, 0.0, op0=MULT, op1=ADD
-        )
+        woven_v = keep.tile([P, X_VECTOR, PACK], BF16, name="woven_v", align_bytes=64)
+        picked_s = keep.tile([P, PACK, S - X_VECTOR], BF16, name="picked_s", align_bytes=64)
+        woven_s = keep.tile([P, S - X_VECTOR, PACK], BF16, name="woven_s", align_bytes=64)
         w_grouped = keep.tile([P, N, PACK], BF16, name="w_grouped", align_bytes=64)
+        for j in range(PACK):
+            nc.vector.tensor_copy(woven_v[:, :, j], planes[j][:].indirect(entries(0, X_VECTOR)))
+            nc.scalar.activation(picked_s[:, j, :], planes[j][:].indirect(entries(X_VECTOR, S)), COPY)
+        nc.scalar.copy(out=woven_s[:], in_=picked_s[:].rearrange("p j s -> p s j"))
         nc.scalar.copy(out=w_grouped[:], in_=w_raw[:].rearrange("p j m -> p m j"))
 
-        def quantize(source, width, name, tag):
-            codes = keep.tile([P, width], U32, name=f"{name}_codes", tag=tag, align_bytes=256)
+        def quantize(source, width, name):
+            codes = keep.tile([P, width], U32, name=f"{name}_codes", align_bytes=256)
             scales = keep.tile([P, width], U8, name=f"{name}_scales", align_bytes=64)
             nc.vector.quantize_mx(
                 out=codes[:].bitcast(FP8X4), scales=scales[:], in_=source.rearrange("p c j -> p (c j)")
             )
             return codes, scales
 
-        quarter0 = quantize(grouped[0][:, PIECE:, :], PIECE, "x0", "x0_codes")
-        w_codes, w_scales = quantize(w_grouped[:], N, "w", "w_codes")
-        quarter1 = quantize(grouped[0][:, :PIECE, :], PIECE, "x1", "w_then_codes")
-        half1 = quantize(grouped[1][:], HALF, "x2", "x2_codes")
+        banks = [psum.tile([P, BANK], F32, name=f"bank{b}") for b in range(S // BANK)]
 
-        banks = []
-        for b, (x_codes, x_scales) in enumerate((quarter0, quarter1, half1)):
-            bank = psum.tile([P, x_codes.shape[1]], F32, name=f"bank{b}")
+        def product(lo, hi, x_codes, x_scales):
             nc.tensor.matmul_mx(
-                out=bank[:],
+                out=banks[lo // BANK][:, lo % BANK : lo % BANK + hi - lo],
                 lhsT=w_codes[:].bitcast(FP8X4),
                 lhsT_scale=w_scales[:],
                 rhs=x_codes[:].bitcast(FP8X4),
@@ -105,36 +83,40 @@ def tile_picked_sidegate_silu_l_kernel(tc, xT, side, w1, offs, out):
                 start=True,
                 stop=True,
             )
-            banks.append(bank)
-        y_first = keep.tile([P, HALF - LATE], F32, name="y_first", tag="pair_then_y")
-        nc.vector.tensor_copy(y_first[:], banks[0][:, LATE - PIECE :])
 
-        gate_rows = keep.tile([P, T], F32, name="gate_rows")
-        for cols in chunks[:-1]:
-            nc.scalar.activation(gate_rows[:, cols], side_rows[:, cols], SILU, bias=zero[:])
-        nc.scalar.activation(gate_rows[:, chunks[-1]], side_rows[:, chunks[-1]], SILU)
+        part_s = quantize(woven_s[:], S - X_VECTOR, "xs")
+        w_codes, w_scales = quantize(w_grouped[:], N, "w")
+        part0 = quantize(woven_v[:, :BANK, :], BANK, "x0")
+        part1 = quantize(woven_v[:, BANK:, :], X_VECTOR - BANK, "x1")
+        product(X_VECTOR, S, *part_s)
+        product(0, BANK, *part0)
+        product(BANK, X_VECTOR, *part1)
 
-        y_second = keep.tile([P, LATE], F32, name="y_second", tag="zero_then_y")
-        nc.scalar.copy(out=y_second[:, PIECE:], in_=banks[0][:, : LATE - PIECE])
-        nc.scalar.copy(out=y_second[:, MIDDLE:PIECE], in_=banks[1][:, MIDDLE:])
-        nc.scalar.copy(out=y_second[:, :MIDDLE], in_=banks[1][:, :MIDDLE])
+        picked = {}
 
-        picked = keep.tile([P, HALF], F32, name="picked")
-        nc.vector.tensor_copy(picked[:], side_rows[:].indirect(halves[1]))
+        def look_up_vector(lo, hi):
+            picked[lo] = keep.tile([P, hi - lo], F32, name=f"picked{lo}")
+            nc.vector.tensor_copy(picked[lo][:], side_rows[:].indirect(entries(lo, hi)))
 
-        def fused_piece(lo, hi, y, tag):
-            res = keep.tile([P, hi - lo], F32, name=f"res{lo}", tag=tag, align_bytes=256)
-            piece = offsets[:, lo // GROUP : hi // GROUP]
-            nc.vector.tensor_tensor(res[:], gate_rows[:].indirect(piece), y, MULT)
+        def look_up_scalar(lo, hi):
+            picked[lo] = keep.tile([P, hi - lo], F32, name=f"picked{lo}")
+            nc.scalar.activation(picked[lo][:], side_rows[:].indirect(entries(lo, hi)), COPY)
+
+        def finish(lo, hi):
+            gate = keep.tile([P, hi - lo], F32, name=f"gate{lo}")
+            nc.scalar.activation(gate[:], picked[lo][:], SILU)
+            res = keep.tile([P, hi - lo], F32, name=f"res{lo}", align_bytes=256)
+            y = banks[lo // BANK][:, lo % BANK : lo % BANK + hi - lo]
+            nc.vector.tensor_tensor(res[:], y, gate[:], MULT)
             nc.sync.dma_start(out=out[:, lo:hi], in_=res[:])
 
-        fused_piece(LATE, HALF, y_first[:], "res352")
-        fused_piece(MIDDLE, LATE, y_second[:, MIDDLE:], "res192")
-        for lo in range(HALF, S, PIECE):
-            cols = slice(lo - HALF, lo - HALF + PIECE)
-            gate = keep.tile([P, PIECE], F32, name=f"gate{lo}", tag=f"gate{lo}", align_bytes=256)
-            nc.scalar.activation(gate[:], picked[:, cols], SILU)
-            res = keep.tile([P, PIECE], F32, name=f"res{lo}", align_bytes=256)
-            nc.vector.tensor_tensor(res[:], banks[2][:, cols], gate[:], MULT)
-            nc.sync.dma_start(out=out[:, lo : lo + PIECE], in_=res[:])
-        fused_piece(0, MIDDLE, y_second[:, :MIDDLE], f"gate{HALF}")
+        look_up_vector(*VECTOR_PIECES[0])
+        look_up_vector(*VECTOR_PIECES[1])
+        look_up_scalar(*SCALAR_PIECES[0])
+        finish(*VECTOR_PIECES[0])
+        finish(*SCALAR_PIECES[0])
+        look_up_scalar(*SCALAR_PIECES[1])
+        finish(*VECTOR_PIECES[1])
+        look_up_scalar(*SCALAR_PIECES[2])
+        finish(*SCALAR_PIECES[1])
+        finish(*SCALAR_PIECES[2])

@@ -14,14 +14,13 @@ FP8X4 = mybir.dt.float8_e4m3fn_x4
 SILU = mybir.ActivationFunctionType.Silu
 COPY = mybir.ActivationFunctionType.Copy
 MULT = mybir.AluOpType.mult
+ADD = mybir.AluOpType.add
 
 P = 128
 PACK = 4
 GROUP = 16
 BANK = 512
 X_VECTOR = 768
-VECTOR_PIECES = ((0, 256), (256, 512))
-SCALAR_PIECES = ((512, 768), (768, 896), (896, 1024))
 
 
 def tile_picked_sidegate_silu_l_kernel(tc, xT, side, w1, offs, out):
@@ -61,7 +60,7 @@ def tile_picked_sidegate_silu_l_kernel(tc, xT, side, w1, offs, out):
             nc.vector.tensor_copy(woven_v[:, :, j], planes[j][:].indirect(entries(0, X_VECTOR)))
             nc.scalar.activation(picked_s[:, j, :], planes[j][:].indirect(entries(X_VECTOR, S)), COPY)
         nc.scalar.copy(out=woven_s[:], in_=picked_s[:].rearrange("p j s -> p s j"))
-        nc.scalar.copy(out=w_grouped[:], in_=w_raw[:].rearrange("p j m -> p m j"))
+        nc.gpsimd.tensor_scalar(w_grouped[:], w_raw[:].rearrange("p j m -> p m j"), 1.0, 0.0, op0=MULT, op1=ADD)
 
         def quantize(source, width, name):
             codes = keep.tile([P, width], U32, name=f"{name}_codes", align_bytes=256)
@@ -84,39 +83,44 @@ def tile_picked_sidegate_silu_l_kernel(tc, xT, side, w1, offs, out):
                 stop=True,
             )
 
-        part_s = quantize(woven_s[:], S - X_VECTOR, "xs")
         w_codes, w_scales = quantize(w_grouped[:], N, "w")
         part0 = quantize(woven_v[:, :BANK, :], BANK, "x0")
         part1 = quantize(woven_v[:, BANK:, :], X_VECTOR - BANK, "x1")
-        product(X_VECTOR, S, *part_s)
+        part_s = quantize(woven_s[:], S - X_VECTOR, "xs")
         product(0, BANK, *part0)
         product(BANK, X_VECTOR, *part1)
+        product(X_VECTOR, S, *part_s)
 
-        picked = {}
+        picked = keep.tile([P, S], F32, name="picked")
+        gates = keep.tile([P, S], F32, name="gates")
+        results = keep.tile([P, S], F32, name="results", align_bytes=256)
 
         def look_up_vector(lo, hi):
-            picked[lo] = keep.tile([P, hi - lo], F32, name=f"picked{lo}")
-            nc.vector.tensor_copy(picked[lo][:], side_rows[:].indirect(entries(lo, hi)))
+            nc.vector.tensor_copy(picked[:, lo:hi], side_rows[:].indirect(entries(lo, hi)))
 
         def look_up_scalar(lo, hi):
-            picked[lo] = keep.tile([P, hi - lo], F32, name=f"picked{lo}")
-            nc.scalar.activation(picked[lo][:], side_rows[:].indirect(entries(lo, hi)), COPY)
+            nc.scalar.activation(picked[:, lo:hi], side_rows[:].indirect(entries(lo, hi)), COPY)
+
+        def gate(lo, hi):
+            nc.scalar.activation(gates[:, lo:hi], picked[:, lo:hi], SILU)
 
         def finish(lo, hi):
-            gate = keep.tile([P, hi - lo], F32, name=f"gate{lo}")
-            nc.scalar.activation(gate[:], picked[lo][:], SILU)
-            res = keep.tile([P, hi - lo], F32, name=f"res{lo}", align_bytes=256)
             y = banks[lo // BANK][:, lo % BANK : lo % BANK + hi - lo]
-            nc.vector.tensor_tensor(res[:], y, gate[:], MULT)
-            nc.sync.dma_start(out=out[:, lo:hi], in_=res[:])
+            nc.vector.tensor_tensor(results[:, lo:hi], y, gates[:, lo:hi], MULT)
+            nc.sync.dma_start(out=out[:, lo:hi], in_=results[:, lo:hi])
 
-        look_up_vector(*VECTOR_PIECES[0])
-        look_up_vector(*VECTOR_PIECES[1])
-        look_up_scalar(*SCALAR_PIECES[0])
-        finish(*VECTOR_PIECES[0])
-        finish(*SCALAR_PIECES[0])
-        look_up_scalar(*SCALAR_PIECES[1])
-        finish(*VECTOR_PIECES[1])
-        look_up_scalar(*SCALAR_PIECES[2])
-        finish(*SCALAR_PIECES[1])
-        finish(*SCALAR_PIECES[2])
+        look_up_vector(0, 256)
+        look_up_vector(256, 640)
+        look_up_scalar(640, 832)
+        gate(0, 256)
+        finish(0, 128)
+        finish(128, 256)
+        look_up_scalar(832, 1024)
+        gate(640, 832)
+        finish(640, 832)
+        gate(256, 512)
+        finish(256, 512)
+        gate(512, 640)
+        finish(512, 640)
+        gate(832, 1024)
+        finish(832, 1024)

@@ -36,12 +36,12 @@ def tile_picked_sidegate_silu_l_kernel(tc, xT, side, w1, offs, out):
         side_rows = keep.tile([P, T], F32, name="side_rows", align_bytes=256)
 
         nc.scalar.dma_start(out=planes[0][:], in_=x_rows[:, 0, :])
+        nc.scalar.dma_start(out=w_raw[:], in_=w1.rearrange("(p j) m -> p j m", j=PACK))
         nc.sync.dma_start(out=planes[1][:], in_=x_rows[:, 1, :])
         nc.sync.dma_start(offsets[:], offs)
         nc.scalar.dma_start(out=planes[2][:, : T // 2], in_=x_rows[:, 2, : T // 2])
         nc.sync.dma_start(out=planes[2][:, T // 2 :], in_=x_rows[:, 2, T // 2 :])
         nc.sync.dma_start(out=planes[3][:], in_=x_rows[:, 3, :])
-        nc.sync.dma_start(out=w_raw[:], in_=w1.rearrange("(p j) m -> p j m", j=PACK))
         nc.sync.dma_start(out=side_rows[:], in_=side)
 
         zero = keep.tile([P, 1], F32, name="zero")
@@ -60,7 +60,7 @@ def tile_picked_sidegate_silu_l_kernel(tc, xT, side, w1, offs, out):
             nc.vector.tensor_copy(woven_v[:, :, j], planes[j][:].indirect(entries(0, X_VECTOR)))
             nc.scalar.activation(picked_s[:, j, :], planes[j][:].indirect(entries(X_VECTOR, S)), COPY)
         nc.scalar.copy(out=woven_s[:], in_=picked_s[:].rearrange("p j s -> p s j"))
-        nc.gpsimd.tensor_scalar(w_grouped[:], w_raw[:].rearrange("p j m -> p m j"), 1.0, 0.0, op0=MULT, op1=ADD)
+        nc.scalar.copy(out=w_grouped[:], in_=w_raw[:].rearrange("p j m -> p m j"))
 
         def quantize(source, width, name):
             codes = keep.tile([P, width], U32, name=f"{name}_codes", align_bytes=256)
@@ -104,23 +104,22 @@ def tile_picked_sidegate_silu_l_kernel(tc, xT, side, w1, offs, out):
         def gate(lo, hi):
             nc.scalar.activation(gates[:, lo:hi], picked[:, lo:hi], SILU)
 
-        def finish(lo, hi):
+        def multiply(lo, hi):
             y = banks[lo // BANK][:, lo % BANK : lo % BANK + hi - lo]
             nc.vector.tensor_tensor(results[:, lo:hi], y, gates[:, lo:hi], MULT)
+
+        def store(lo, hi):
             nc.sync.dma_start(out=out[:, lo:hi], in_=results[:, lo:hi])
 
-        look_up_vector(0, 256)
-        look_up_vector(256, 640)
-        look_up_scalar(640, 832)
-        gate(0, 256)
-        finish(0, 128)
-        finish(128, 256)
-        look_up_scalar(832, 1024)
-        gate(640, 832)
-        finish(640, 832)
-        gate(256, 512)
-        finish(256, 512)
-        gate(512, 640)
-        finish(512, 640)
-        gate(832, 1024)
-        finish(832, 1024)
+        look_up_vector(128, 512)
+        look_up_scalar(0, 128)
+        look_up_vector(768, 1024)
+        look_up_scalar(512, 768)
+        for lo, hi in ((0, 128), (128, 320), (320, 512), (512, 768)):
+            gate(lo, hi)
+            multiply(lo, hi)
+            store(lo, hi)
+        for lo, hi in ((768, 896), (896, 1024)):
+            gate(lo, hi)
+            multiply(lo, hi)
+        store(768, 1024)

@@ -115,11 +115,9 @@ def tile_picked_sidegate_silu_l_kernel(tc, xT, side, w1, offs, out):
         look_up_scalar(0, 128)
         look_up_vector(768, 1024)
         look_up_scalar(512, 768)
-        for lo, hi in ((0, 128), (128, 320), (320, 512), (512, 768)):
-            gate(lo, hi)
-            multiply(lo, hi)
-            store(lo, hi)
-        for lo, hi in ((768, 896), (896, 1024)):
-            gate(lo, hi)
-            multiply(lo, hi)
-        store(768, 1024)
+        stores = {128: 0, 256: 128, 512: 256, 768: 512, 1024: 768}
+        for lo in range(0, S, 128):
+            gate(lo, lo + 128)
+            multiply(lo, lo + 128)
+            if lo + 128 in stores:
+                store(stores[lo + 128], lo + 128)

@@ -21,6 +21,7 @@ PACK = 4
 GROUP = 16
 BANK = 512
 X_VECTOR = 768
+PLANE2_CUT = 1024
 
 
 def tile_picked_sidegate_silu_l_kernel(tc, xT, side, w1, offs, out):
@@ -39,8 +40,8 @@ def tile_picked_sidegate_silu_l_kernel(tc, xT, side, w1, offs, out):
         nc.scalar.dma_start(out=w_raw[:], in_=w1.rearrange("(p j) m -> p j m", j=PACK))
         nc.sync.dma_start(out=planes[1][:], in_=x_rows[:, 1, :])
         nc.sync.dma_start(offsets[:], offs)
-        nc.scalar.dma_start(out=planes[2][:, : T // 2], in_=x_rows[:, 2, : T // 2])
-        nc.sync.dma_start(out=planes[2][:, T // 2 :], in_=x_rows[:, 2, T // 2 :])
+        nc.scalar.dma_start(out=planes[2][:, :PLANE2_CUT], in_=x_rows[:, 2, :PLANE2_CUT])
+        nc.sync.dma_start(out=planes[2][:, PLANE2_CUT:], in_=x_rows[:, 2, PLANE2_CUT:])
         nc.sync.dma_start(out=planes[3][:], in_=x_rows[:, 3, :])
         nc.sync.dma_start(out=side_rows[:], in_=side)
 

@@ -14,7 +14,6 @@ FP8X4 = mybir.dt.float8_e4m3fn_x4
 SILU = mybir.ActivationFunctionType.Silu
 COPY = mybir.ActivationFunctionType.Copy
 MULT = mybir.AluOpType.mult
-ADD = mybir.AluOpType.add
 
 P = 128
 PACK = 4
@@ -22,6 +21,7 @@ GROUP = 16
 BANK = 512
 X_VECTOR = 768
 PLANE2_CUT = 1024
+POOL_SHARE = 128
 
 
 def tile_picked_sidegate_silu_l_kernel(tc, xT, side, w1, offs, out):
@@ -36,12 +36,16 @@ def tile_picked_sidegate_silu_l_kernel(tc, xT, side, w1, offs, out):
         w_raw = keep.tile([P, PACK, N], F32, name="w_raw", align_bytes=256)
         side_rows = keep.tile([P, T], F32, name="side_rows", align_bytes=256)
 
-        nc.scalar.dma_start(out=planes[0][:], in_=x_rows[:, 0, :])
+        nc.scalar.dma_start(out=planes[0][:, : T // 2], in_=x_rows[:, 0, : T // 2])
+        nc.scalar.dma_start(out=planes[0][:, T // 2 :], in_=x_rows[:, 0, T // 2 :])
         nc.scalar.dma_start(out=w_raw[:], in_=w1.rearrange("(p j) m -> p j m", j=PACK))
-        nc.sync.dma_start(out=planes[1][:], in_=x_rows[:, 1, :])
+        nc.sync.dma_start(out=planes[1][:, : T // 2], in_=x_rows[:, 1, : T // 2])
+        nc.sync.dma_start(out=planes[1][:, T // 2 :], in_=x_rows[:, 1, T // 2 :])
         nc.sync.dma_start(offsets[:], offs)
         nc.scalar.dma_start(out=planes[2][:, :PLANE2_CUT], in_=x_rows[:, 2, :PLANE2_CUT])
-        nc.sync.dma_start(out=planes[2][:, PLANE2_CUT:], in_=x_rows[:, 2, PLANE2_CUT:])
+        nc.sync.dma_start(out=planes[2][:, PLANE2_CUT : T // 2], in_=x_rows[:, 2, PLANE2_CUT : T // 2])
+        nc.sync.dma_start(out=planes[2][:, T // 2 : 3 * T // 4], in_=x_rows[:, 2, T // 2 : 3 * T // 4])
+        nc.sync.dma_start(out=planes[2][:, 3 * T // 4 :], in_=x_rows[:, 2, 3 * T // 4 :])
         nc.sync.dma_start(out=planes[3][:], in_=x_rows[:, 3, :])
         nc.sync.dma_start(out=side_rows[:], in_=side)
 
@@ -72,25 +76,31 @@ def tile_picked_sidegate_silu_l_kernel(tc, xT, side, w1, offs, out):
             return codes, scales
 
         banks = [psum.tile([P, BANK], F32, name=f"bank{b}") for b in range(S // BANK)]
+        first_bank = psum.tile([P, POOL_SHARE], F32, name="first_bank")
 
-        def product(lo, hi, x_codes, x_scales):
+        def product(target, x_codes, x_scales):
             nc.tensor.matmul_mx(
-                out=banks[lo // BANK][:, lo % BANK : lo % BANK + hi - lo],
+                out=target,
                 lhsT=w_codes[:].bitcast(FP8X4),
                 lhsT_scale=w_scales[:],
-                rhs=x_codes[:].bitcast(FP8X4),
-                rhs_scale=x_scales[:],
+                rhs=x_codes.bitcast(FP8X4),
+                rhs_scale=x_scales,
                 start=True,
                 stop=True,
             )
 
         w_codes, w_scales = quantize(w_grouped[:], N, "w")
-        part0 = quantize(woven_v[:, :BANK, :], BANK, "x0")
-        part1 = quantize(woven_v[:, BANK:, :], X_VECTOR - BANK, "x1")
-        part_s = quantize(woven_s[:], S - X_VECTOR, "xs")
-        product(0, BANK, *part0)
-        product(BANK, X_VECTOR, *part1)
-        product(X_VECTOR, S, *part_s)
+        codes, scales = quantize(woven_v[:, :POOL_SHARE, :], POOL_SHARE, "xp")
+        product(first_bank[:], codes[:], scales[:])
+        codes, scales = quantize(woven_v[:, POOL_SHARE:BANK, :], BANK - POOL_SHARE, "x0")
+        product(banks[0][:, 128:384], codes[:, :256], scales[:, :256])
+        product(banks[0][:, 384:], codes[:, 256:], scales[:, 256:])
+        codes, scales = quantize(woven_v[:, BANK:, :], X_VECTOR - BANK, "x1")
+        product(banks[1][:, : X_VECTOR - BANK], codes[:], scales[:])
+        codes, scales = quantize(woven_s[:], S - X_VECTOR, "xs")
+        product(banks[1][:, X_VECTOR - BANK :], codes[:], scales[:])
+        y_copy = keep.tile([P, POOL_SHARE], F32, name="y_copy")
+        nc.scalar.copy(out=y_copy[:], in_=first_bank[:])
 
         picked = keep.tile([P, S], F32, name="picked")
         gates = keep.tile([P, S], F32, name="gates")
@@ -112,12 +122,15 @@ def tile_picked_sidegate_silu_l_kernel(tc, xT, side, w1, offs, out):
         def store(lo, hi):
             nc.sync.dma_start(out=out[:, lo:hi], in_=results[:, lo:hi])
 
-        look_up_vector(128, 512)
+        look_up_vector(256, 640)
         look_up_scalar(0, 128)
         look_up_vector(768, 1024)
-        look_up_scalar(512, 768)
-        stores = {128: 0, 256: 128, 512: 256, 768: 512, 1024: 768}
-        for lo in range(0, S, 128):
+        look_up_scalar(128, 256)
+        gate(0, 128)
+        nc.gpsimd.tensor_tensor(results[:, :POOL_SHARE], y_copy[:], gates[:, :POOL_SHARE], MULT)
+        look_up_scalar(640, 768)
+        stores = {256: 0, 512: 256, 768: 512, 1024: 768}
+        for lo in range(128, S, 128):
             gate(lo, lo + 128)
             multiply(lo, lo + 128)
             if lo + 128 in stores:

@@ -14,6 +14,7 @@ FP8X4 = mybir.dt.float8_e4m3fn_x4
 SILU = mybir.ActivationFunctionType.Silu
 COPY = mybir.ActivationFunctionType.Copy
 MULT = mybir.AluOpType.mult
+ADD = mybir.AluOpType.add
 
 P = 128
 PACK = 4
@@ -21,7 +22,6 @@ GROUP = 16
 BANK = 512
 X_VECTOR = 768
 PLANE2_CUT = 1024
-POOL_SHARE = 128
 
 
 def tile_picked_sidegate_silu_l_kernel(tc, xT, side, w1, offs, out):
@@ -44,8 +44,7 @@ def tile_picked_sidegate_silu_l_kernel(tc, xT, side, w1, offs, out):
         nc.sync.dma_start(offsets[:], offs)
         nc.scalar.dma_start(out=planes[2][:, :PLANE2_CUT], in_=x_rows[:, 2, :PLANE2_CUT])
         nc.sync.dma_start(out=planes[2][:, PLANE2_CUT : T // 2], in_=x_rows[:, 2, PLANE2_CUT : T // 2])
-        nc.sync.dma_start(out=planes[2][:, T // 2 : 3 * T // 4], in_=x_rows[:, 2, T // 2 : 3 * T // 4])
-        nc.sync.dma_start(out=planes[2][:, 3 * T // 4 :], in_=x_rows[:, 2, 3 * T // 4 :])
+        nc.sync.dma_start(out=planes[2][:, T // 2 :], in_=x_rows[:, 2, T // 2 :])
         nc.sync.dma_start(out=planes[3][:], in_=x_rows[:, 3, :])
         nc.sync.dma_start(out=side_rows[:], in_=side)
 
@@ -76,31 +75,25 @@ def tile_picked_sidegate_silu_l_kernel(tc, xT, side, w1, offs, out):
             return codes, scales
 
         banks = [psum.tile([P, BANK], F32, name=f"bank{b}") for b in range(S // BANK)]
-        first_bank = psum.tile([P, POOL_SHARE], F32, name="first_bank")
 
-        def product(target, x_codes, x_scales):
+        def product(lo, hi, x_codes, x_scales):
             nc.tensor.matmul_mx(
-                out=target,
+                out=banks[lo // BANK][:, lo % BANK : lo % BANK + hi - lo],
                 lhsT=w_codes[:].bitcast(FP8X4),
                 lhsT_scale=w_scales[:],
-                rhs=x_codes.bitcast(FP8X4),
-                rhs_scale=x_scales,
+                rhs=x_codes[:].bitcast(FP8X4),
+                rhs_scale=x_scales[:],
                 start=True,
                 stop=True,
             )
 
         w_codes, w_scales = quantize(w_grouped[:], N, "w")
-        codes, scales = quantize(woven_v[:, :POOL_SHARE, :], POOL_SHARE, "xp")
-        product(first_bank[:], codes[:], scales[:])
-        codes, scales = quantize(woven_v[:, POOL_SHARE:BANK, :], BANK - POOL_SHARE, "x0")
-        product(banks[0][:, 128:384], codes[:, :256], scales[:, :256])
-        product(banks[0][:, 384:], codes[:, 256:], scales[:, 256:])
-        codes, scales = quantize(woven_v[:, BANK:, :], X_VECTOR - BANK, "x1")
-        product(banks[1][:, : X_VECTOR - BANK], codes[:], scales[:])
-        codes, scales = quantize(woven_s[:], S - X_VECTOR, "xs")
-        product(banks[1][:, X_VECTOR - BANK :], codes[:], scales[:])
-        y_copy = keep.tile([P, POOL_SHARE], F32, name="y_copy")
-        nc.scalar.copy(out=y_copy[:], in_=first_bank[:])
+        part0 = quantize(woven_v[:, :BANK, :], BANK, "x0")
+        part1 = quantize(woven_v[:, BANK:, :], X_VECTOR - BANK, "x1")
+        part_s = quantize(woven_s[:], S - X_VECTOR, "xs")
+        product(0, BANK, *part0)
+        product(BANK, X_VECTOR, *part1)
+        product(X_VECTOR, S, *part_s)
 
         picked = keep.tile([P, S], F32, name="picked")
         gates = keep.tile([P, S], F32, name="gates")
@@ -122,15 +115,12 @@ def tile_picked_sidegate_silu_l_kernel(tc, xT, side, w1, offs, out):
         def store(lo, hi):
             nc.sync.dma_start(out=out[:, lo:hi], in_=results[:, lo:hi])
 
-        look_up_vector(256, 640)
+        look_up_vector(128, 512)
         look_up_scalar(0, 128)
         look_up_vector(768, 1024)
-        look_up_scalar(128, 256)
-        gate(0, 128)
-        nc.gpsimd.tensor_tensor(results[:, :POOL_SHARE], y_copy[:], gates[:, :POOL_SHARE], MULT)
-        look_up_scalar(640, 768)
-        stores = {256: 0, 512: 256, 768: 512, 1024: 768}
-        for lo in range(128, S, 128):
+        look_up_scalar(512, 768)
+        stores = {128: 0, 256: 128, 512: 256, 768: 512, 1024: 768}
+        for lo in range(0, S, 128):
             gate(lo, lo + 128)
             multiply(lo, lo + 128)
             if lo + 128 in stores:

@@ -14,13 +14,12 @@ FP8X4 = mybir.dt.float8_e4m3fn_x4
 SILU = mybir.ActivationFunctionType.Silu
 COPY = mybir.ActivationFunctionType.Copy
 MULT = mybir.AluOpType.mult
-ADD = mybir.AluOpType.add
 
 P = 128
 PACK = 4
 GROUP = 16
 BANK = 512
-X_VECTOR = 768
+X_VECTOR = 640
 PLANE2_CUT = 1024
 
 
@@ -76,13 +75,13 @@ def tile_picked_sidegate_silu_l_kernel(tc, xT, side, w1, offs, out):
 
         banks = [psum.tile([P, BANK], F32, name=f"bank{b}") for b in range(S // BANK)]
 
-        def product(lo, hi, x_codes, x_scales):
+        def product(lo, hi, first, x_codes, x_scales):
             nc.tensor.matmul_mx(
                 out=banks[lo // BANK][:, lo % BANK : lo % BANK + hi - lo],
                 lhsT=w_codes[:].bitcast(FP8X4),
                 lhsT_scale=w_scales[:],
-                rhs=x_codes[:].bitcast(FP8X4),
-                rhs_scale=x_scales[:],
+                rhs=x_codes[:, lo - first : hi - first].bitcast(FP8X4),
+                rhs_scale=x_scales[:, lo - first : hi - first],
                 start=True,
                 stop=True,
             )
@@ -91,9 +90,10 @@ def tile_picked_sidegate_silu_l_kernel(tc, xT, side, w1, offs, out):
         part0 = quantize(woven_v[:, :BANK, :], BANK, "x0")
         part1 = quantize(woven_v[:, BANK:, :], X_VECTOR - BANK, "x1")
         part_s = quantize(woven_s[:], S - X_VECTOR, "xs")
-        product(0, BANK, *part0)
-        product(BANK, X_VECTOR, *part1)
-        product(X_VECTOR, S, *part_s)
+        product(0, BANK, 0, *part0)
+        product(BANK, X_VECTOR, BANK, *part1)
+        product(X_VECTOR, 768, X_VECTOR, *part_s)
+        product(768, S, X_VECTOR, *part_s)
 
         picked = keep.tile([P, S], F32, name="picked")
         gates = keep.tile([P, S], F32, name="gates")

from contextlib import ExitStack

import concourse.mybir as mybir

K, T, S, N = 512, 4096, 1024, 128
FLOPS = 2 * K * S * N

F32 = mybir.dt.float32
BF16 = mybir.dt.bfloat16
U32 = mybir.dt.uint32
U16 = mybir.dt.uint16
U8 = mybir.dt.uint8
FP8X4 = mybir.dt.float8_e4m3fn_x4
SILU = mybir.ActivationFunctionType.Silu
COPY = mybir.ActivationFunctionType.Copy
MULT = mybir.AluOpType.mult

P = 128
PACK = 4
GROUP = 16
BANK = 512
X_VECTOR = 640
PLANE2_CUT = 1024


def tile_picked_sidegate_silu_l_kernel(tc, xT, side, w1, offs, out):
    nc = tc.nc
    with ExitStack() as ctx:
        keep = ctx.enter_context(tc.tile_pool(name="keep", bufs=1))
        psum = ctx.enter_context(tc.psum_pool(name="psum", bufs=1))

        offsets = keep.tile([P, S // GROUP], U16, name="offsets")
        x_rows = xT.rearrange("(p j) t -> p j t", j=PACK)
        planes = [keep.tile([P, T], F32, name=f"plane{j}", align_bytes=256) for j in range(PACK)]
        w_raw = keep.tile([P, PACK, N], F32, name="w_raw", align_bytes=256)
        side_rows = keep.tile([P, T], F32, name="side_rows", align_bytes=256)

        nc.scalar.dma_start(out=planes[0][:, : T // 2], in_=x_rows[:, 0, : T // 2])
        nc.scalar.dma_start(out=planes[0][:, T // 2 :], in_=x_rows[:, 0, T // 2 :])
        nc.scalar.dma_start(out=w_raw[:], in_=w1.rearrange("(p j) m -> p j m", j=PACK))
        nc.sync.dma_start(out=planes[1][:, : T // 2], in_=x_rows[:, 1, : T // 2])
        nc.sync.dma_start(out=planes[1][:, T // 2 :], in_=x_rows[:, 1, T // 2 :])
        nc.sync.dma_start(offsets[:], offs)
        nc.scalar.dma_start(out=planes[2][:, :PLANE2_CUT], in_=x_rows[:, 2, :PLANE2_CUT])
        nc.sync.dma_start(out=planes[2][:, PLANE2_CUT : T // 2], in_=x_rows[:, 2, PLANE2_CUT : T // 2])
        nc.sync.dma_start(out=planes[2][:, T // 2 :], in_=x_rows[:, 2, T // 2 :])
        nc.sync.dma_start(out=planes[3][:], in_=x_rows[:, 3, :])
        nc.sync.dma_start(out=side_rows[:], in_=side)

        zero = keep.tile([P, 1], F32, name="zero")
        nc.vector.memset(zero[:], 0.0)
        warm_out = keep.tile([P, 1], F32, name="warm_out")
        nc.scalar.activation(warm_out[:], zero[:], SILU)

        def entries(lo, hi):
            return offsets[:, lo // GROUP : hi // GROUP]

        woven_v = keep.tile([P, X_VECTOR, PACK], BF16, name="woven_v", align_bytes=64)
        picked_s = keep.tile([P, PACK, S - X_VECTOR], BF16, name="picked_s", align_bytes=64)
        woven_s = keep.tile([P, S - X_VECTOR, PACK], BF16, name="woven_s", align_bytes=64)
        w_grouped = keep.tile([P, N, PACK], BF16, name="w_grouped", align_bytes=64)
        for j in range(PACK):
            nc.vector.tensor_copy(woven_v[:, :, j], planes[j][:].indirect(entries(0, X_VECTOR)))
            nc.scalar.activation(picked_s[:, j, :], planes[j][:].indirect(entries(X_VECTOR, S)), COPY)
        nc.scalar.copy(out=woven_s[:], in_=picked_s[:].rearrange("p j s -> p s j"))
        nc.scalar.copy(out=w_grouped[:], in_=w_raw[:].rearrange("p j m -> p m j"))

        def quantize(source, width, name):
            codes = keep.tile([P, width], U32, name=f"{name}_codes", align_bytes=256)
            scales = keep.tile([P, width], U8, name=f"{name}_scales", align_bytes=64)
            nc.vector.quantize_mx(
                out=codes[:].bitcast(FP8X4), scales=scales[:], in_=source.rearrange("p c j -> p (c j)")
            )
            return codes, scales

        banks = [psum.tile([P, BANK], F32, name=f"bank{b}") for b in range(S // BANK)]

        def product(lo, hi, first, x_codes, x_scales):
            nc.tensor.matmul_mx(
                out=banks[lo // BANK][:, lo % BANK : lo % BANK + hi - lo],
                lhsT=w_codes[:].bitcast(FP8X4),
                lhsT_scale=w_scales[:],
                rhs=x_codes[:, lo - first : hi - first].bitcast(FP8X4),
                rhs_scale=x_scales[:, lo - first : hi - first],
                start=True,
                stop=True,
            )

        w_codes, w_scales = quantize(w_grouped[:], N, "w")
        part0 = quantize(woven_v[:, :BANK, :], BANK, "x0")
        part1 = quantize(woven_v[:, BANK:, :], X_VECTOR - BANK, "x1")
        part_s = quantize(woven_s[:], S - X_VECTOR, "xs")
        product(0, BANK, 0, *part0)
        product(BANK, X_VECTOR, BANK, *part1)
        product(X_VECTOR, 768, X_VECTOR, *part_s)
        product(768, S, X_VECTOR, *part_s)

        picked = keep.tile([P, S], F32, name="picked")
        gates = keep.tile([P, S], F32, name="gates")
        results = keep.tile([P, S], F32, name="results", align_bytes=256)

        def look_up_vector(lo, hi):
            nc.vector.tensor_copy(picked[:, lo:hi], side_rows[:].indirect(entries(lo, hi)))

        def look_up_scalar(lo, hi):
            nc.scalar.activation(picked[:, lo:hi], side_rows[:].indirect(entries(lo, hi)), COPY)

        def gate(lo, hi):
            nc.scalar.activation(gates[:, lo:hi], picked[:, lo:hi], SILU)

        def multiply(lo, hi):
            y = banks[lo // BANK][:, lo % BANK : lo % BANK + hi - lo]
            nc.vector.tensor_tensor(results[:, lo:hi], y, gates[:, lo:hi], MULT)

        def store(lo, hi):
            nc.sync.dma_start(out=out[:, lo:hi], in_=results[:, lo:hi])

        look_up_vector(128, 512)
        look_up_scalar(0, 128)
        look_up_vector(768, 1024)
        look_up_scalar(512, 768)
        stores = {128: 0, 256: 128, 512: 256, 768: 512, 1024: 768}
        for lo in range(0, S, 128):
            gate(lo, lo + 128)
            multiply(lo, lo + 128)
            if lo + 128 in stores:
                store(stores[lo + 128], lo + 128)
